import numpy as np
import ml_dtypes


def mxq(x, axis, fmt="e4m3"):
    dtype, down = {"e4m3": (ml_dtypes.float8_e4m3fn, 7), "e5m2": (ml_dtypes.float8_e5m2, 14)}[fmt]
    v = np.moveaxis(np.asarray(x, np.float32).astype(ml_dtypes.bfloat16).astype(np.float64), axis, -1)
    blocks = v.reshape(v.shape[:-1] + (-1, 32))
    amax = np.abs(blocks).max(-1, keepdims=True)
    byte = np.maximum(np.where(amax > 0, np.frexp(amax)[1] - 1 + 127, 0) - down, 1)
    scale = np.exp2(byte - 127.0)
    codes = (blocks / scale).astype(np.float32).astype(dtype).astype(np.float64)
    return np.moveaxis((codes * scale).reshape(v.shape), -1, axis)


WIDE = False


def mx_kscale(k):
    if not WIDE:
        return np.ones(k)
    levels = np.array([10, -10, 5, -5, 0])
    if k % 512:
        return np.exp2(np.random.permutation(np.resize(levels, k // 32))).repeat(32)
    a = np.empty((k // 512, 16))
    for p in range(k // 512):
        a[p, :8] = np.random.permutation(np.resize(levels, 8))
        for g in range(8):
            far = levels[np.abs(levels - a[p, g]) >= 10]
            a[p, g + 8] = far[np.random.randint(len(far))]
    return np.exp2(a.ravel()).repeat(32)


def f64(x):
    return np.asarray(x).astype(np.float64)


def striped(idx):
    return np.tile(idx.reshape(-1, 16).T, (8, 1)).astype(np.uint16)


def unstriped(offs):
    return offs[:16].T.reshape(-1).astype(np.int64)


def striped8(idx):
    return np.concatenate([x.reshape(-1, 16).T for x in idx]).astype(np.uint16)


def runs(offs, k):
    lists = np.stack([offs[16 * r : 16 * r + 16].T.reshape(-1) for r in range(8)]).astype(np.int64)
    return lists[np.arange(k) % 512 // 64]


def pack_weight(w):
    k, n = w.shape
    w = f64(np.asarray(w, np.float32).astype(ml_dtypes.bfloat16)).reshape(k // 32, 32, n)
    amax = np.abs(w).max(1)
    byte = np.clip(np.where(amax > 0, np.frexp(amax)[1] - 1 + 127 - 7, 1), 1, 254)
    scaled = (w * np.exp2(127.0 - byte)[:, None, :]).reshape(k, n).astype(np.float32)
    words = np.ascontiguousarray(scaled.reshape(k // 512, 128, 4, n).transpose(0, 1, 3, 2)).astype(ml_dtypes.float8_e4m3fn).view(np.uint8)
    return words, np.ascontiguousarray(byte.astype(np.uint8).reshape(k // 512, 16, n))


def unpack_weight(words, scales):
    g, p, n, _ = words.shape
    vals = np.ascontiguousarray(words).view(ml_dtypes.float8_e4m3fn).astype(np.float64) * np.repeat(np.exp2(scales.astype(np.float64) - 127.0), 8, axis=1)[..., None]
    return vals.transpose(0, 1, 3, 2).reshape(g * 512, n)


K, T, S, N, H = 512, 2048, 512, 512, 512


def setup_inputs():
    n = np.random.standard_normal
    s = mx_kscale(K)[:, None]
    u = mx_kscale(S)
    packed_xT = pack_weight(n((K, T)) * s)
    return {
        "x_words": packed_xT[0],
        "x_scales": packed_xT[1],
        "wa": (n((K, H)) / np.sqrt(K) / s).astype(np.float32),
        "wb": (n((K, H)) / np.sqrt(K) / s).astype(np.float32),
        "gt": (np.random.uniform(0.5, 1.5, (S, 1)) * u[:, None]).astype(np.float32),
        "w1": (n((S, N)) / np.sqrt(S) / u[:, None]).astype(np.float32),
        "offs": striped(np.random.permutation(T)[:S]),
        "two": striped(np.random.permutation(T)[:S]),
        "n1": striped8(np.stack([np.random.permutation(H) for _ in range(8)])),
        "n2": striped8(np.stack([np.random.permutation(H) for _ in range(8)])),
        "n3": striped8(np.stack([np.random.permutation(H) for _ in range(8)])),
        "n4": striped8(np.stack([np.random.permutation(H) for _ in range(8)])),
        "n5": striped8(np.stack([np.random.permutation(H) for _ in range(8)])),
    }


def reference(x_words, x_scales, wa, wb, gt, w1, offs, two, n1, n2, n3, n4, n5):
    xq = unpack_weight(x_words, x_scales)[:, unstriped(offs)]
    y = xq.T @ mxq(f64(wa), 0, "e4m3")
    x_two = unpack_weight(x_words, x_scales)[:, unstriped(two)]
    d = x_two.T @ mxq(f64(wb), 0, "e4m3")
    z = f64(gt) * (np.maximum(np.minimum(y - (0.5 * (y[np.arange(S)[:, None], runs(n1, S)])), d[np.arange(S)[:, None], runs(n2, S)]), d[np.arange(S)[:, None], runs(n3, S)]))
    h = mxq(f64(w1), 0, "e4m3").T @ mxq(z, 0, "e4m3")
    return 0.75 * ((h - (h[np.arange(N)[:, None], runs(n4, N)])) * (h - (h[np.arange(N)[:, None], runs(n5, N)])))

@@ -1,0 +1,219 @@
+from contextlib import ExitStack
+
+import concourse.mybir as mybir
+
+K, T, S, N, H = 512, 2048, 512, 512, 512
+FLOPS = 2 * K * S * H * 2 + 2 * S * N * H
+
+F32 = mybir.dt.float32
+BF16 = mybir.dt.bfloat16
+I32 = mybir.dt.int32
+U32 = mybir.dt.uint32
+U16 = mybir.dt.uint16
+U8 = mybir.dt.uint8
+FP8X4 = mybir.dt.float8_e4m3fn_x4
+ALU = mybir.AluOpType
+ACT = mybir.ActivationFunctionType
+
+P = 128
+PACK = 4
+HALF = H // 2
+LANES = 16
+
+
+def tile_picked_twtclampbquad_none_p_kernel(
+    tc, x_words, x_scales, wa, wb, gt, w1, offs, two, n1, n2, n3, n4, n5, out
+):
+    nc = tc.nc
+    with ExitStack() as ctx:
+        keep = ctx.enter_context(tc.tile_pool(name="keep", bufs=1))
+        psum = ctx.enter_context(tc.psum_pool(name="psum", bufs=1))
+
+        def load_list(src, name):
+            tile = keep.tile([P, S // LANES], U16, name=name)
+            nc.sync.dma_start(tile[:], src)
+            return tile
+
+        def load_rows(src, name):
+            raw = keep.tile([P, PACK, src.shape[1]], F32, name=name)
+            nc.sync.dma_start(raw[:], src.rearrange("(p j) w -> p j w", j=PACK))
+            return raw
+
+        def quantize(grouped, width, name):
+            codes = keep.tile([P, width], U32, name=name + "_codes", align_bytes=64)
+            scales = keep.tile([P, width], U8, name=name + "_scales", align_bytes=64)
+            nc.vector.quantize_mx(out=codes[:].bitcast(FP8X4), scales=scales[:], in_=grouped)
+            return codes, scales
+
+        def matmul(acc, lhs, cols, rhs):
+            nc.tensor.matmul_mx(
+                out=acc,
+                lhsT=lhs[0][:, cols].bitcast(FP8X4),
+                lhsT_scale=lhs[1][:, cols],
+                rhs=rhs[0][:].bitcast(FP8X4),
+                rhs_scale=rhs[1][:],
+                start=True,
+                stop=True,
+            )
+
+        def interleave(copy, dst, src):
+            copy(
+                dst.rearrange("p (c i) t -> p c t i", i=4),
+                src.rearrange("p t (c i) -> p c t i", i=4),
+            )
+
+        x_byte = keep.tile([P, T], U8, name="x_byte")
+        nc.gpsimd.memset(x_byte[:].bitcast(I32), 0)
+        for q in range(4):
+            nc.sync.dma_start(
+                x_byte[32 * q : 32 * q + 4, :].bitcast(I32), x_scales[0, 4 * q : 4 * q + 4, :].bitcast(I32)
+            )
+        two_l = load_list(two, "two_l")
+        offs_l = load_list(offs, "offs_l")
+        wb_raw = load_rows(wb, "wb_raw")
+        x_word = keep.tile([P, T], I32, name="x_word")
+        nc.sync.dma_start(x_word[:], x_words[0].rearrange("p n t -> p (n t)").bitcast(I32))
+        gt_sb = keep.tile([P, PACK], F32, name="gt_sb")
+        nc.sync.dma_start(gt_sb[:], gt.rearrange("(p j) o -> p (j o)", j=PACK))
+        n2_l = load_list(n2, "n2_l")
+        wa_raw = load_rows(wa, "wa_raw")
+        n3_l = load_list(n3, "n3_l")
+        n1_l = load_list(n1, "n1_l")
+        w1_raw = load_rows(w1, "w1_raw")
+        n4_l = load_list(n4, "n4_l")
+        n5_l = load_list(n5, "n5_l")
+
+        d_win = [keep.tile([P, 2 * H], F32, name=f"d_win{t}") for t in range(PACK)]
+        yh_win = [keep.tile([P, 2 * H], F32, name=f"yh_win{t}") for t in range(PACK)]
+        for win in d_win + yh_win:
+            nc.gpsimd.memset(win[:, H:], 0.0)
+
+        gt_abs = keep.tile([P, PACK], F32, name="gt_abs")
+        gt_half = keep.tile([P, PACK], F32, name="gt_half")
+        gt_sign = keep.tile([P, PACK], F32, name="gt_sign")
+        gt_pos = keep.tile([P, PACK], F32, name="gt_pos")
+        nc.gpsimd.tensor_scalar(gt_pos[:], gt_sb[:], 0.0, None, ALU.is_ge)
+        nc.gpsimd.tensor_scalar(gt_sign[:], gt_pos[:], 2.0, -1.0, ALU.mult, ALU.add)
+        nc.gpsimd.tensor_tensor(gt_abs[:], gt_sb[:], gt_sign[:], ALU.mult)
+        nc.gpsimd.tensor_scalar(gt_half[:], gt_abs[:], -0.5, 0.0, ALU.mult, ALU.add)
+
+        def pick_bytes(lst, name):
+            got = keep.tile([P, S], U8, name=name + "_got")
+            nc.vector.tensor_copy(got[:], x_byte[:].indirect(lst[:]))
+            return got
+
+        def deal_bytes(got, name):
+            dealt = keep.tile([P, S], U8, name=name + "_dealt", align_bytes=64)
+            nc.vector.tensor_copy(
+                dealt[:].rearrange("p (t s) -> p t s", t=PACK), got[:].rearrange("p (s t) -> p t s", t=PACK)
+            )
+            return dealt
+
+        def pick_words(lst, name):
+            dealt = keep.tile([P, S], U32, name=name, align_bytes=64)
+            nc.vector.tensor_copy(
+                dealt[:].rearrange("p (t s) -> p s t", t=PACK), x_word[:].bitcast(U32).indirect(lst[:])
+            )
+            return dealt
+
+        two_got = pick_bytes(two_l, "two_b")
+        offs_got = pick_bytes(offs_l, "offs_b")
+        two_bytes = deal_bytes(two_got, "two_b")
+        wb_g = keep.tile([P, H, PACK], BF16, name="wb_g", align_bytes=64)
+        interleave(nc.scalar.copy, wb_g[:, HALF:, :], wb_raw[:, :, HALF:])
+        interleave(nc.vector.tensor_copy, wb_g[:, :HALF, :], wb_raw[:, :, :HALF])
+        offs_bytes = deal_bytes(offs_got, "offs_b")
+        wb_q = quantize(wb_g[:].rearrange("p w j -> p (w j)"), H, "wb")
+        two_words = pick_words(two_l, "two_w")
+        offs_words = pick_words(offs_l, "offs_w")
+
+        banks = [psum.tile([P, H], F32, name=f"bank{b}") for b in range(8)]
+        rows = [slice(t * P, (t + 1) * P) for t in range(PACK)]
+
+        for t in range(PACK):
+            matmul(banks[t][:], (two_words, two_bytes), rows[t], wb_q)
+        wa_g = keep.tile([P, H, PACK], BF16, name="wa_g", align_bytes=64)
+        quarter = H // PACK
+        for t in range(PACK):
+            nc.scalar.activation(d_win[t][:, :H], banks[t][:], ACT.Copy, scale=gt_abs[:, t : t + 1])
+            cols = slice(t * quarter, (t + 1) * quarter)
+            interleave(nc.scalar.copy, wa_g[:, cols, :], wa_raw[:, :, cols])
+
+        d2 = keep.tile([P, PACK, H], BF16, name="d2")
+        for t in range(PACK):
+            nc.vector.tensor_copy(d2[:, t, :], d_win[t][:].indirect(n2_l[:]))
+        wa_q = quantize(wa_g[:].rearrange("p w j -> p (w j)"), H, "wa")
+
+        w1_s = keep.tile([P, PACK, N], BF16, name="w1_s")
+        for j in range(PACK):
+            nc.gpsimd.tensor_scalar(w1_s[:, j, :], w1_raw[:, j, :], gt_sign[:, j : j + 1], 0.0, ALU.mult, ALU.add)
+
+        list_half = [slice(0, HALF // LANES), slice(HALF // LANES, H // LANES)]
+        col_half = [slice(0, HALF), slice(HALF, H)]
+        d3a = keep.tile([P, PACK, HALF], BF16, name="d3a")
+        for t in range(PACK):
+            nc.vector.tensor_copy(d3a[:, t, :], d_win[t][:].indirect(n3_l[:, list_half[0]]))
+
+        y_sb = [keep.tile([P, H], F32, name=f"y_sb{t}") for t in range(PACK)]
+        a32 = [keep.tile([P, H], F32, name=f"a32_{t}") for t in range(PACK)]
+        a16 = keep.tile([P, PACK - 1, H], BF16, name="a16")
+        for t in range(PACK):
+            matmul(banks[PACK + t][:], (offs_words, offs_bytes), rows[t], wa_q)
+        for t in range(PACK):
+            nc.scalar.activation(yh_win[t][:, :H], banks[PACK + t][:], ACT.Copy, scale=gt_half[:, t : t + 1])
+            nc.scalar.activation(y_sb[t][:], banks[PACK + t][:], ACT.Copy, scale=gt_abs[:, t : t + 1])
+        for t in range(PACK):
+            nc.vector.tensor_tensor(a32[t][:], yh_win[t][:].indirect(n1_l[:]), y_sb[t][:], ALU.add)
+            if t < PACK - 1:
+                nc.scalar.copy(a16[:, t, :], a32[t][:])
+
+        w1_g = keep.tile([P, N, PACK], BF16, name="w1_g", align_bytes=64)
+        nc.scalar.copy(
+            w1_g[:].rearrange("p (t m) j -> p m t j", t=PACK), w1_s[:].rearrange("p j (m t) -> p m t j", t=PACK)
+        )
+
+        low = keep.tile([P, PACK, H], BF16, name="low")
+        nc.vector.tensor_tensor(low[:, : PACK - 1, :], a16[:], d2[:, : PACK - 1, :], ALU.min)
+        nc.vector.tensor_tensor(low[:, PACK - 1, :], a32[PACK - 1][:], d2[:, PACK - 1, :], ALU.min)
+        w1_q = quantize(w1_g[:].rearrange("p w j -> p (w j)"), N, "w1")
+
+        z_rows = [keep.tile([P, PACK, HALF], BF16, name=f"z_rows{c}") for c in range(2)]
+        z_g = [keep.tile([P, HALF, PACK], BF16, name=f"z_g{c}", align_bytes=64) for c in range(2)]
+        nc.vector.tensor_tensor(z_rows[0][:], low[:, :, col_half[0]], d3a[:], ALU.max)
+        interleave(nc.scalar.copy, z_g[0][:], z_rows[0][:])
+        d3b = a32[PACK - 1][:].bitcast(BF16).rearrange("p (t j) -> p t j", t=PACK)
+        for t in range(PACK):
+            nc.vector.tensor_copy(d3b[:, t, :], d_win[t][:].indirect(n3_l[:, list_half[1]]))
+        z_q = [quantize(z_g[0][:].rearrange("p w j -> p (w j)"), HALF, "za")]
+        nc.vector.tensor_tensor(z_rows[1][:], low[:, :, col_half[1]], d3b, ALU.max)
+        interleave(nc.vector.tensor_copy, z_g[1][:], z_rows[1][:])
+        z_q.append(quantize(z_g[1][:].rearrange("p w j -> p (w j)"), HALF, "zb"))
+
+        h_sb = [keep.tile([P, H], F32, name=f"h_sb{t}") for t in range(PACK)]
+        for c in range(2):
+            for t in range(PACK):
+                acc = banks[PACK * c + t][:, :HALF]
+                matmul(acc, w1_q, rows[t], z_q[c])
+                nc.scalar.copy(yh_win[t][:, col_half[c]], acc)
+                nc.scalar.copy(h_sb[t][:, col_half[c]], acc)
+
+        out_rows = out.rearrange("(p t) j -> p t j", t=PACK)
+        pieces = [(t, slice(0, H)) for t in range(PACK - 1)] + [(PACK - 1, col_half[0]), (PACK - 1, col_half[1])]
+        made = []
+
+        def finish(t, cols, diff4, diff5, res):
+            nc.vector.scalar_tensor_tensor(res[:], diff4[:], 0.75, diff5[:], ALU.mult, ALU.mult)
+            nc.sync.dma_start(out_rows[:, t, cols], res[:])
+
+        for u, (t, cols) in enumerate(pieces):
+            width = cols.stop - cols.start
+            entries = slice(cols.start // LANES, cols.stop // LANES)
+            diff4 = keep.tile([P, width], F32, name=f"diff4_{u}")
+            diff5 = keep.tile([P, width], F32, name=f"diff5_{u}")
+            res = keep.tile([P, width], F32, name=f"res{u}")
+            nc.vector.tensor_tensor(diff4[:], yh_win[t][:].indirect(n4_l[:, entries]), h_sb[t][:, cols], ALU.subtract)
+            if made:
+                finish(*made[-1])
+            nc.vector.tensor_tensor(diff5[:], yh_win[t][:].indirect(n5_l[:, entries]), h_sb[t][:, cols], ALU.subtract)
+            made.append((t, cols, diff4, diff5, res))
+        finish(*made[-1])

@@ -27,6 +27,7 @@ def tile_picked_twtclampbquad_none_p_kernel(
     nc = tc.nc
     with ExitStack() as ctx:
         keep = ctx.enter_context(tc.tile_pool(name="keep", bufs=1))
+        reuse = ctx.enter_context(tc.tile_pool(name="reuse", bufs=1))
         psum = ctx.enter_context(tc.psum_pool(name="psum", bufs=1))
 
         def load_list(src, name):
@@ -109,8 +110,8 @@ def tile_picked_twtclampbquad_none_p_kernel(
             )
             return dealt
 
-        def pick_words(lst, name):
-            dealt = keep.tile([P, S], U32, name=name, align_bytes=64)
+        def pick_words(lst, name, offset):
+            dealt = reuse.tile([P, S], U32, name=name, align_bytes=64, offset=offset)
             nc.vector.tensor_copy(
                 dealt[:].rearrange("p (t s) -> p s t", t=PACK), x_word[:].bitcast(U32).indirect(lst[:])
             )
@@ -119,43 +120,48 @@ def tile_picked_twtclampbquad_none_p_kernel(
         two_got = pick_bytes(two_l, "two_b")
         offs_got = pick_bytes(offs_l, "offs_b")
         two_bytes = deal_bytes(two_got, "two_b")
-        wb_g = keep.tile([P, H, PACK], BF16, name="wb_g", align_bytes=64)
+        wb_g = reuse.tile([P, H, PACK], BF16, name="wb_g", align_bytes=64, offset=0)
         interleave(nc.scalar.copy, wb_g[:, HALF:, :], wb_raw[:, :, HALF:])
         interleave(nc.vector.tensor_copy, wb_g[:, :HALF, :], wb_raw[:, :, :HALF])
         offs_bytes = deal_bytes(offs_got, "offs_b")
         wb_q = quantize(wb_g[:].rearrange("p w j -> p (w j)"), H, "wb")
-        two_words = pick_words(two_l, "two_w")
-        offs_words = pick_words(offs_l, "offs_w")
+        two_words = pick_words(two_l, "two_w", 0)
+        offs_words = pick_words(offs_l, "offs_w", 4 * S)
 
         banks = [psum.tile([P, H], F32, name=f"bank{b}") for b in range(8)]
         rows = [slice(t * P, (t + 1) * P) for t in range(PACK)]
 
         for t in range(PACK):
             matmul(banks[t][:], (two_words, two_bytes), rows[t], wb_q)
-        wa_g = keep.tile([P, H, PACK], BF16, name="wa_g", align_bytes=64)
-        quarter = H // PACK
-        for t in range(PACK):
+        wa_g = keep.tile([P, H, PACK], BF16, name="wa_g", tag="wa_g", align_bytes=64)
+        col_half = [slice(0, HALF), slice(HALF, H)]
+
+        def copy_d(t):
             nc.scalar.activation(d_win[t][:, :H], banks[t][:], ACT.Copy, scale=gt_abs[:, t : t + 1])
-            cols = slice(t * quarter, (t + 1) * quarter)
-            interleave(nc.scalar.copy, wa_g[:, cols, :], wa_raw[:, :, cols])
+
+        copy_d(0)
+        copy_d(1)
+        for c in range(2):
+            interleave(nc.scalar.copy, wa_g[:, col_half[c], :], wa_raw[:, :, col_half[c]])
+            copy_d(2 + c)
 
         d2 = keep.tile([P, PACK, H], BF16, name="d2")
-        for t in range(PACK):
+        for t in range(PACK - 1):
             nc.vector.tensor_copy(d2[:, t, :], d_win[t][:].indirect(n2_l[:]))
         wa_q = quantize(wa_g[:].rearrange("p w j -> p (w j)"), H, "wa")
+        nc.vector.tensor_copy(d2[:, PACK - 1, :], d_win[PACK - 1][:].indirect(n2_l[:]))
 
         w1_s = keep.tile([P, PACK, N], BF16, name="w1_s")
         for j in range(PACK):
             nc.gpsimd.tensor_scalar(w1_s[:, j, :], w1_raw[:, j, :], gt_sign[:, j : j + 1], 0.0, ALU.mult, ALU.add)
 
         list_half = [slice(0, HALF // LANES), slice(HALF // LANES, H // LANES)]
-        col_half = [slice(0, HALF), slice(HALF, H)]
-        d3a = keep.tile([P, PACK, HALF], BF16, name="d3a")
+        d3a = keep.tile([P, PACK, HALF], BF16, name="d3a", tag="wa_g", align_bytes=64)
         for t in range(PACK):
             nc.vector.tensor_copy(d3a[:, t, :], d_win[t][:].indirect(n3_l[:, list_half[0]]))
 
         y_sb = [keep.tile([P, H], F32, name=f"y_sb{t}") for t in range(PACK)]
-        a32 = [keep.tile([P, H], F32, name=f"a32_{t}") for t in range(PACK)]
+        a32 = [keep.tile([P, H], F32, name=f"a32_{t}", tag=f"a32_{t}", align_bytes=64) for t in range(PACK)]
         a16 = keep.tile([P, PACK - 1, H], BF16, name="a16")
         for t in range(PACK):
             matmul(banks[PACK + t][:], (offs_words, offs_bytes), rows[t], wa_q)
@@ -167,38 +173,49 @@ def tile_picked_twtclampbquad_none_p_kernel(
             if t < PACK - 1:
                 nc.scalar.copy(a16[:, t, :], a32[t][:])
 
-        w1_g = keep.tile([P, N, PACK], BF16, name="w1_g", align_bytes=64)
-        nc.scalar.copy(
-            w1_g[:].rearrange("p (t m) j -> p m t j", t=PACK), w1_s[:].rearrange("p j (m t) -> p m t j", t=PACK)
-        )
+        w1_g = keep.tile([P, PACK, P, PACK], BF16, name="w1_g", tag=f"a32_{PACK - 2}", align_bytes=64)
+        nc.scalar.copy(w1_g[:].rearrange("p t m j -> p m t j"), w1_s[:].rearrange("p j (m t) -> p m t j", t=PACK))
 
         low = keep.tile([P, PACK, H], BF16, name="low")
         nc.vector.tensor_tensor(low[:, : PACK - 1, :], a16[:], d2[:, : PACK - 1, :], ALU.min)
         nc.vector.tensor_tensor(low[:, PACK - 1, :], a32[PACK - 1][:], d2[:, PACK - 1, :], ALU.min)
-        w1_q = quantize(w1_g[:].rearrange("p w j -> p (w j)"), N, "w1")
 
-        z_rows = [keep.tile([P, PACK, HALF], BF16, name=f"z_rows{c}") for c in range(2)]
-        z_g = [keep.tile([P, HALF, PACK], BF16, name=f"z_g{c}", align_bytes=64) for c in range(2)]
-        nc.vector.tensor_tensor(z_rows[0][:], low[:, :, col_half[0]], d3a[:], ALU.max)
-        interleave(nc.scalar.copy, z_g[0][:], z_rows[0][:])
+        z_rows0 = keep.tile([P, PACK, HALF], BF16, name="z_rows0")
+        z_g0 = keep.tile([P, HALF, PACK], BF16, name="z_g0", tag="z_g0", align_bytes=64)
+        nc.vector.tensor_tensor(z_rows0[:], low[:, :, col_half[0]], d3a[:], ALU.max)
+        interleave(nc.scalar.copy, z_g0[:], z_rows0[:])
         d3b = a32[PACK - 1][:].bitcast(BF16).rearrange("p (t j) -> p t j", t=PACK)
         for t in range(PACK):
             nc.vector.tensor_copy(d3b[:, t, :], d_win[t][:].indirect(n3_l[:, list_half[1]]))
-        z_q = [quantize(z_g[0][:].rearrange("p w j -> p (w j)"), HALF, "za")]
-        nc.vector.tensor_tensor(z_rows[1][:], low[:, :, col_half[1]], d3b, ALU.max)
-        interleave(nc.vector.tensor_copy, z_g[1][:], z_rows[1][:])
-        z_q.append(quantize(z_g[1][:].rearrange("p w j -> p (w j)"), HALF, "zb"))
+        z_q = [quantize(z_g0[:].rearrange("p w j -> p (w j)"), HALF, "za")]
+        z_rows1 = keep.tile([P, PACK, HALF], BF16, name="z_rows1", tag="z_g0", align_bytes=64)
+        z_g1 = keep.tile([P, HALF, PACK], BF16, name="z_g1", tag="z_g1", align_bytes=64)
+        nc.vector.tensor_tensor(z_rows1[:], low[:, :, col_half[1]], d3b, ALU.max)
+        w1_first = quantize(w1_g[:, 0, :, :].rearrange("p m j -> p (m j)"), P, "w1_first")
+        interleave(nc.vector.tensor_copy, z_g1[:], z_rows1[:])
+        z_q.append(quantize(z_g1[:].rearrange("p w j -> p (w j)"), HALF, "zb"))
+        rest_codes = keep.tile([P, N - P], U32, name="rest_codes", tag="z_g1", align_bytes=64)
+        rest_scales = keep.tile([P, N - P], U8, name="rest_scales", align_bytes=64)
+        for t0, t1 in ((1, 2), (2, PACK)):
+            cols = slice((t0 - 1) * P, (t1 - 1) * P)
+            nc.vector.quantize_mx(
+                out=rest_codes[:, cols].bitcast(FP8X4),
+                scales=rest_scales[:, cols],
+                in_=w1_g[:, t0:t1, :, :].rearrange("p t m j -> p (t m j)"),
+            )
+        w1_parts = [(w1_first, rows[0])] + [((rest_codes, rest_scales), rows[t]) for t in range(PACK - 1)]
 
         h_sb = [keep.tile([P, H], F32, name=f"h_sb{t}") for t in range(PACK)]
-        for c in range(2):
-            for t in range(PACK):
+        for t in range(PACK):
+            for c in range(2):
                 acc = banks[PACK * c + t][:, :HALF]
-                matmul(acc, w1_q, rows[t], z_q[c])
+                matmul(acc, w1_parts[t][0], w1_parts[t][1], z_q[c])
                 nc.scalar.copy(yh_win[t][:, col_half[c]], acc)
                 nc.scalar.copy(h_sb[t][:, col_half[c]], acc)
 
         out_rows = out.rearrange("(p t) j -> p t j", t=PACK)
-        pieces = [(t, slice(0, H)) for t in range(PACK - 1)] + [(PACK - 1, col_half[0]), (PACK - 1, col_half[1])]
+        pieces = [(0, col_half[0]), (0, col_half[1]), (1, slice(0, H)), (2, slice(0, H))]
+        pieces = pieces + [(PACK - 1, col_half[0]), (PACK - 1, col_half[1])]
         made = []
 
         def finish(t, cols, diff4, diff5, res):

from contextlib import ExitStack

import concourse.mybir as mybir

K, T, S, N, H = 512, 2048, 512, 512, 512
FLOPS = 2 * K * S * H * 2 + 2 * S * N * H

F32 = mybir.dt.float32
BF16 = mybir.dt.bfloat16
I32 = mybir.dt.int32
U32 = mybir.dt.uint32
U16 = mybir.dt.uint16
U8 = mybir.dt.uint8
FP8X4 = mybir.dt.float8_e4m3fn_x4
ALU = mybir.AluOpType
ACT = mybir.ActivationFunctionType

P = 128
PACK = 4
HALF = H // 2
LANES = 16


def tile_picked_twtclampbquad_none_p_kernel(
    tc, x_words, x_scales, wa, wb, gt, w1, offs, two, n1, n2, n3, n4, n5, out
):
    nc = tc.nc
    with ExitStack() as ctx:
        keep = ctx.enter_context(tc.tile_pool(name="keep", bufs=1))
        reuse = ctx.enter_context(tc.tile_pool(name="reuse", bufs=1))
        psum = ctx.enter_context(tc.psum_pool(name="psum", bufs=1))

        def load_list(src, name):
            tile = keep.tile([P, S // LANES], U16, name=name)
            nc.sync.dma_start(tile[:], src)
            return tile

        def load_rows(src, name):
            raw = keep.tile([P, PACK, src.shape[1]], F32, name=name)
            nc.sync.dma_start(raw[:], src.rearrange("(p j) w -> p j w", j=PACK))
            return raw

        def quantize(grouped, width, name):
            codes = keep.tile([P, width], U32, name=name + "_codes", align_bytes=64)
            scales = keep.tile([P, width], U8, name=name + "_scales", align_bytes=64)
            nc.vector.quantize_mx(out=codes[:].bitcast(FP8X4), scales=scales[:], in_=grouped)
            return codes, scales

        def matmul(acc, lhs, cols, rhs):
            nc.tensor.matmul_mx(
                out=acc,
                lhsT=lhs[0][:, cols].bitcast(FP8X4),
                lhsT_scale=lhs[1][:, cols],
                rhs=rhs[0][:].bitcast(FP8X4),
                rhs_scale=rhs[1][:],
                start=True,
                stop=True,
            )

        def interleave(copy, dst, src):
            copy(
                dst.rearrange("p (c i) t -> p c t i", i=4),
                src.rearrange("p t (c i) -> p c t i", i=4),
            )

        x_byte = keep.tile([P, T], U8, name="x_byte")
        nc.gpsimd.memset(x_byte[:].bitcast(I32), 0)
        for q in range(4):
            nc.sync.dma_start(
                x_byte[32 * q : 32 * q + 4, :].bitcast(I32), x_scales[0, 4 * q : 4 * q + 4, :].bitcast(I32)
            )
        two_l = load_list(two, "two_l")
        offs_l = load_list(offs, "offs_l")
        wb_raw = load_rows(wb, "wb_raw")
        x_word = keep.tile([P, T], I32, name="x_word")
        nc.sync.dma_start(x_word[:], x_words[0].rearrange("p n t -> p (n t)").bitcast(I32))
        gt_sb = keep.tile([P, PACK], F32, name="gt_sb")
        nc.sync.dma_start(gt_sb[:], gt.rearrange("(p j) o -> p (j o)", j=PACK))
        n2_l = load_list(n2, "n2_l")
        wa_raw = load_rows(wa, "wa_raw")
        n3_l = load_list(n3, "n3_l")
        n1_l = load_list(n1, "n1_l")
        w1_raw = load_rows(w1, "w1_raw")
        n4_l = load_list(n4, "n4_l")
        n5_l = load_list(n5, "n5_l")

        d_win = [keep.tile([P, 2 * H], F32, name=f"d_win{t}") for t in range(PACK)]
        yh_win = [keep.tile([P, 2 * H], F32, name=f"yh_win{t}") for t in range(PACK)]
        for win in d_win + yh_win:
            nc.gpsimd.memset(win[:, H:], 0.0)

        gt_abs = keep.tile([P, PACK], F32, name="gt_abs")
        gt_half = keep.tile([P, PACK], F32, name="gt_half")
        gt_sign = keep.tile([P, PACK], F32, name="gt_sign")
        gt_pos = keep.tile([P, PACK], F32, name="gt_pos")
        nc.gpsimd.tensor_scalar(gt_pos[:], gt_sb[:], 0.0, None, ALU.is_ge)
        nc.gpsimd.tensor_scalar(gt_sign[:], gt_pos[:], 2.0, -1.0, ALU.mult, ALU.add)
        nc.gpsimd.tensor_tensor(gt_abs[:], gt_sb[:], gt_sign[:], ALU.mult)
        nc.gpsimd.tensor_scalar(gt_half[:], gt_abs[:], -0.5, 0.0, ALU.mult, ALU.add)

        def pick_bytes(lst, name):
            got = keep.tile([P, S], U8, name=name + "_got")
            nc.vector.tensor_copy(got[:], x_byte[:].indirect(lst[:]))
            return got

        def deal_bytes(got, name):
            dealt = keep.tile([P, S], U8, name=name + "_dealt", align_bytes=64)
            nc.vector.tensor_copy(
                dealt[:].rearrange("p (t s) -> p t s", t=PACK), got[:].rearrange("p (s t) -> p t s", t=PACK)
            )
            return dealt

        def pick_words(lst, name, offset):
            dealt = reuse.tile([P, S], U32, name=name, align_bytes=64, offset=offset)
            nc.vector.tensor_copy(
                dealt[:].rearrange("p (t s) -> p s t", t=PACK), x_word[:].bitcast(U32).indirect(lst[:])
            )
            return dealt

        two_got = pick_bytes(two_l, "two_b")
        offs_got = pick_bytes(offs_l, "offs_b")
        two_bytes = deal_bytes(two_got, "two_b")
        wb_g = reuse.tile([P, H, PACK], BF16, name="wb_g", align_bytes=64, offset=0)
        interleave(nc.scalar.copy, wb_g[:, HALF:, :], wb_raw[:, :, HALF:])
        interleave(nc.vector.tensor_copy, wb_g[:, :HALF, :], wb_raw[:, :, :HALF])
        offs_bytes = deal_bytes(offs_got, "offs_b")
        wb_q = quantize(wb_g[:].rearrange("p w j -> p (w j)"), H, "wb")
        two_words = pick_words(two_l, "two_w", 0)
        offs_words = pick_words(offs_l, "offs_w", 4 * S)

        banks = [psum.tile([P, H], F32, name=f"bank{b}") for b in range(8)]
        rows = [slice(t * P, (t + 1) * P) for t in range(PACK)]

        for t in range(PACK):
            matmul(banks[t][:], (two_words, two_bytes), rows[t], wb_q)
        wa_g = keep.tile([P, H, PACK], BF16, name="wa_g", tag="wa_g", align_bytes=64)
        col_half = [slice(0, HALF), slice(HALF, H)]

        def copy_d(t):
            nc.scalar.activation(d_win[t][:, :H], banks[t][:], ACT.Copy, scale=gt_abs[:, t : t + 1])

        copy_d(0)
        copy_d(1)
        for c in range(2):
            interleave(nc.scalar.copy, wa_g[:, col_half[c], :], wa_raw[:, :, col_half[c]])
            copy_d(2 + c)

        d2 = keep.tile([P, PACK, H], BF16, name="d2")
        for t in range(PACK - 1):
            nc.vector.tensor_copy(d2[:, t, :], d_win[t][:].indirect(n2_l[:]))
        wa_q = quantize(wa_g[:].rearrange("p w j -> p (w j)"), H, "wa")
        nc.vector.tensor_copy(d2[:, PACK - 1, :], d_win[PACK - 1][:].indirect(n2_l[:]))

        w1_s = keep.tile([P, PACK, N], BF16, name="w1_s")
        for j in range(PACK):
            nc.gpsimd.tensor_scalar(w1_s[:, j, :], w1_raw[:, j, :], gt_sign[:, j : j + 1], 0.0, ALU.mult, ALU.add)

        list_half = [slice(0, HALF // LANES), slice(HALF // LANES, H // LANES)]
        d3a = keep.tile([P, PACK, HALF], BF16, name="d3a", tag="wa_g", align_bytes=64)
        for t in range(PACK):
            nc.vector.tensor_copy(d3a[:, t, :], d_win[t][:].indirect(n3_l[:, list_half[0]]))

        y_sb = [keep.tile([P, H], F32, name=f"y_sb{t}") for t in range(PACK)]
        a32 = [keep.tile([P, H], F32, name=f"a32_{t}", tag=f"a32_{t}", align_bytes=64) for t in range(PACK)]
        a16 = keep.tile([P, PACK - 1, H], BF16, name="a16")
        for t in range(PACK):
            matmul(banks[PACK + t][:], (offs_words, offs_bytes), rows[t], wa_q)
        for t in range(PACK):
            nc.scalar.activation(yh_win[t][:, :H], banks[PACK + t][:], ACT.Copy, scale=gt_half[:, t : t + 1])
            nc.scalar.activation(y_sb[t][:], banks[PACK + t][:], ACT.Copy, scale=gt_abs[:, t : t + 1])
        for t in range(PACK):
            nc.vector.tensor_tensor(a32[t][:], yh_win[t][:].indirect(n1_l[:]), y_sb[t][:], ALU.add)
            if t < PACK - 1:
                nc.scalar.copy(a16[:, t, :], a32[t][:])

        w1_g = keep.tile([P, PACK, P, PACK], BF16, name="w1_g", tag=f"a32_{PACK - 2}", align_bytes=64)
        nc.scalar.copy(w1_g[:].rearrange("p t m j -> p m t j"), w1_s[:].rearrange("p j (m t) -> p m t j", t=PACK))

        low = keep.tile([P, PACK, H], BF16, name="low")
        nc.vector.tensor_tensor(low[:, : PACK - 1, :], a16[:], d2[:, : PACK - 1, :], ALU.min)
        nc.vector.tensor_tensor(low[:, PACK - 1, :], a32[PACK - 1][:], d2[:, PACK - 1, :], ALU.min)

        z_rows0 = keep.tile([P, PACK, HALF], BF16, name="z_rows0")
        z_g0 = keep.tile([P, HALF, PACK], BF16, name="z_g0", tag="z_g0", align_bytes=64)
        nc.vector.tensor_tensor(z_rows0[:], low[:, :, col_half[0]], d3a[:], ALU.max)
        interleave(nc.scalar.copy, z_g0[:], z_rows0[:])
        d3b = a32[PACK - 1][:].bitcast(BF16).rearrange("p (t j) -> p t j", t=PACK)
        for t in range(PACK):
            nc.vector.tensor_copy(d3b[:, t, :], d_win[t][:].indirect(n3_l[:, list_half[1]]))
        z_q = [quantize(z_g0[:].rearrange("p w j -> p (w j)"), HALF, "za")]
        z_rows1 = keep.tile([P, PACK, HALF], BF16, name="z_rows1", tag="z_g0", align_bytes=64)
        z_g1 = keep.tile([P, HALF, PACK], BF16, name="z_g1", tag="z_g1", align_bytes=64)
        nc.vector.tensor_tensor(z_rows1[:], low[:, :, col_half[1]], d3b, ALU.max)
        w1_first = quantize(w1_g[:, 0, :, :].rearrange("p m j -> p (m j)"), P, "w1_first")
        interleave(nc.vector.tensor_copy, z_g1[:], z_rows1[:])
        z_q.append(quantize(z_g1[:].rearrange("p w j -> p (w j)"), HALF, "zb"))
        rest_codes = keep.tile([P, N - P], U32, name="rest_codes", tag="z_g1", align_bytes=64)
        rest_scales = keep.tile([P, N - P], U8, name="rest_scales", align_bytes=64)
        for t0, t1 in ((1, 2), (2, PACK)):
            cols = slice((t0 - 1) * P, (t1 - 1) * P)
            nc.vector.quantize_mx(
                out=rest_codes[:, cols].bitcast(FP8X4),
                scales=rest_scales[:, cols],
                in_=w1_g[:, t0:t1, :, :].rearrange("p t m j -> p (t m j)"),
            )
        w1_parts = [(w1_first, rows[0])] + [((rest_codes, rest_scales), rows[t]) for t in range(PACK - 1)]

        h_sb = [keep.tile([P, H], F32, name=f"h_sb{t}") for t in range(PACK)]
        for t in range(PACK):
            for c in range(2):
                acc = banks[PACK * c + t][:, :HALF]
                matmul(acc, w1_parts[t][0], w1_parts[t][1], z_q[c])
                nc.scalar.copy(yh_win[t][:, col_half[c]], acc)
                nc.scalar.copy(h_sb[t][:, col_half[c]], acc)

        out_rows = out.rearrange("(p t) j -> p t j", t=PACK)
        pieces = [(0, col_half[0]), (0, col_half[1]), (1, slice(0, H)), (2, slice(0, H))]
        pieces = pieces + [(PACK - 1, col_half[0]), (PACK - 1, col_half[1])]
        made = []

        def finish(t, cols, diff4, diff5, res):
            nc.vector.scalar_tensor_tensor(res[:], diff4[:], 0.75, diff5[:], ALU.mult, ALU.mult)
            nc.sync.dma_start(out_rows[:, t, cols], res[:])

        for u, (t, cols) in enumerate(pieces):
            width = cols.stop - cols.start
            entries = slice(cols.start // LANES, cols.stop // LANES)
            diff4 = keep.tile([P, width], F32, name=f"diff4_{u}")
            diff5 = keep.tile([P, width], F32, name=f"diff5_{u}")
            res = keep.tile([P, width], F32, name=f"res{u}")
            nc.vector.tensor_tensor(diff4[:], yh_win[t][:].indirect(n4_l[:, entries]), h_sb[t][:, cols], ALU.subtract)
            if made:
                finish(*made[-1])
            nc.vector.tensor_tensor(diff5[:], yh_win[t][:].indirect(n5_l[:, entries]), h_sb[t][:, cols], ALU.subtract)
            made.append((t, cols, diff4, diff5, res))
        finish(*made[-1])
